import numpy as np
import ml_dtypes


def mxq(x, axis, fmt="e4m3"):
    dtype, down = {"e4m3": (ml_dtypes.float8_e4m3fn, 7), "e5m2": (ml_dtypes.float8_e5m2, 14)}[fmt]
    v = np.moveaxis(np.asarray(x, np.float32).astype(ml_dtypes.bfloat16).astype(np.float64), axis, -1)
    blocks = v.reshape(v.shape[:-1] + (-1, 32))
    amax = np.abs(blocks).max(-1, keepdims=True)
    byte = np.maximum(np.where(amax > 0, np.frexp(amax)[1] - 1 + 127, 0) - down, 1)
    scale = np.exp2(byte - 127.0)
    codes = (blocks / scale).astype(np.float32).astype(dtype).astype(np.float64)
    return np.moveaxis((codes * scale).reshape(v.shape), -1, axis)


WIDE = False


def mx_kscale(k):
    if not WIDE:
        return np.ones(k)
    levels = np.array([10, -10, 5, -5, 0])
    if k % 512:
        return np.exp2(np.random.permutation(np.resize(levels, k // 32))).repeat(32)
    a = np.empty((k // 512, 16))
    for p in range(k // 512):
        a[p, :8] = np.random.permutation(np.resize(levels, 8))
        for g in range(8):
            far = levels[np.abs(levels - a[p, g]) >= 10]
            a[p, g + 8] = far[np.random.randint(len(far))]
    return np.exp2(a.ravel()).repeat(32)


def f64(x):
    return np.asarray(x).astype(np.float64)


def striped(idx):
    return np.tile(np.asarray(idx).reshape(-1, 16).T, (8, 1)).astype(np.uint16)


def unstriped(offs):
    return offs[:16].T.reshape(-1).astype(np.int64)


E2M1 = np.array([0.0, 0.5, 1.0, 1.5, 2.0, 3.0, 4.0, 6.0, -0.0, -0.5, -1.0, -1.5, -2.0, -3.0, -4.0, -6.0])


def pack_weight(w, fmt):
    k, n = w.shape
    w = f64(np.asarray(w, np.float32).astype(ml_dtypes.bfloat16)).reshape(k // 32, 32, n)
    amax = np.abs(w).max(1)
    if fmt == "e4m3":
        byte = np.frexp(amax)[1] - 1 + 127 - 7
    else:
        mant, ex = np.frexp(amax / 6.0)
        byte = np.where(mant > 0.5, ex, ex - 1) + 127
    byte = np.clip(np.where(amax > 0, byte, 1), 1, 254)
    scaled = (w * np.exp2(127.0 - byte)[:, None, :]).reshape(k, n).astype(np.float32)
    by_word = np.ascontiguousarray(scaled.reshape(k // 512, 128, 4, n).transpose(0, 1, 3, 2))
    if fmt == "e4m3":
        words = by_word.astype(ml_dtypes.float8_e4m3fn).view(np.uint8)
    else:
        c = by_word.astype(ml_dtypes.float4_e2m1fn).view(np.uint8) & 0xF
        words = (c[..., 0::2] | (c[..., 1::2] << 4)).reshape(k // 512, 128, 2 * n)
    return np.ascontiguousarray(words), np.ascontiguousarray(byte.astype(np.uint8).reshape(k // 512, 16, n))


def unpack_weight(words, scales, fmt):
    g, _, n = scales.shape
    words = np.ascontiguousarray(words).reshape(g, 128, n, -1)
    if fmt == "e4m3":
        vals = words.view(ml_dtypes.float8_e4m3fn).astype(np.float64)
    else:
        nib = np.empty((g, 128, n, 4), np.uint8)
        nib[..., 0::2] = words & 0xF
        nib[..., 1::2] = words >> 4
        vals = E2M1[nib]
    vals = vals * np.repeat(np.exp2(scales.astype(np.float64) - 127.0), 8, axis=1)[..., None]
    return vals.transpose(0, 1, 3, 2).reshape(g * 512, n)


B, N, T, D, DV, NQ = 2, 1024, 4096, 512, 256, 128
PAGE = 512


def setup_inputs():
    n = np.random.standard_normal
    pages = np.random.permutation(T // PAGE)[:B * N // PAGE]
    idx = (pages[:, None] * PAGE + np.arange(PAGE)[None, :]).reshape(-1)
    s = mx_kscale(D)[:, None]
    u = np.ones(T)
    u[idx] = mx_kscale(B * N)
    r = np.random.uniform(0.5, 2.0, T)
    k = n((D, T)) / s
    v = n((DV, T)) / (u * r)
    kp = pack_weight(k, "e4m3")
    vp = pack_weight(v.T, "e4m3")
    return {
        "qT": (n((B, D, NQ)) * s * (0.80 / np.sqrt(D))).astype(np.float32),
        "k_words": kp[0],
        "k_scales": kp[1],
        "v_words": vp[0],
        "v_scales": vp[1],
        "vs": np.tile(u * r, (128, 1)).astype(np.float32),
        "offs": striped(idx),
        "voffs": striped((pages[:, None] * DV + np.arange(DV)[None, :]).reshape(-1)),
    }


def reference(qT, k_words, k_scales, v_words, v_scales, vs, offs, voffs):
    idx = unstriped(offs)
    k = unpack_weight(k_words, k_scales, "e4m3")
    v = unpack_weight(v_words, v_scales, "e4m3")
    v = v.reshape(T // 512, 512, DV)[unstriped(voffs)[::DV] // DV].reshape(B, N, DV)
    pick = lambda x: x[:, idx].reshape(x.shape[0], B, N).transpose(1, 0, 2)
    q = f64(qT)
    score = mxq(q, 1, "e4m3").transpose(0, 2, 1) @ pick(k)
    p = 1.0 / (1.0 + np.exp(-score))
    w = p * pick(f64(vs))[:, :1, :]
    y = mxq(w, 2, "e4m3") @ v
    y = y / 16.0
    return y

@@ -1,0 +1,148 @@
+from contextlib import ExitStack
+
+import concourse.mybir as mybir
+from concourse.masks import make_identity
+
+B, N, T, D, DV, NQ = 2, 1024, 4096, 512, 256, 128
+PAGE = 512
+P = 128
+PACK = 4
+PAGES = B * N // PAGE
+POOL_PAGES = T // PAGE
+FLOPS = 2 * B * NQ * N * (D + DV)
+
+F32 = mybir.dt.float32
+BF16 = mybir.dt.bfloat16
+I32 = mybir.dt.int32
+U32 = mybir.dt.uint32
+U16 = mybir.dt.uint16
+U8 = mybir.dt.uint8
+FP8X4 = mybir.dt.float8_e4m3fn_x4
+ACT = mybir.ActivationFunctionType
+MULT = mybir.AluOpType.mult
+
+
+def tile_attend_pkv8_sigmoid_kernel(tc, qT, k_words, k_scales, v_words, v_scales, vs, offs, voffs, out):
+    nc = tc.nc
+    with ExitStack() as ctx:
+        keep = ctx.enter_context(tc.tile_pool(name="keep", bufs=1))
+        psum = ctx.enter_context(tc.psum_pool(name="psum", bufs=1))
+
+        key_list = keep.tile([P, B * N // 16], U16, name="key_list")
+        val_list = keep.tile([P, PAGES * DV // 16], U16, name="val_list")
+        ks_pool = keep.tile([P, T], U8, name="ks_pool", align_bytes=64)
+        q_raw = keep.tile([P, B, PACK, NQ], F32, name="q_raw", tag="queries_then_token_scales", align_bytes=64)
+        ident = keep.tile([P, P], F32, name="ident", align_bytes=64)
+        warm = keep.tile([P, 8], F32, name="warm", tag="warm_then_value_scales", align_bytes=64)
+        warm_out = keep.tile([P, 8], F32, name="warm_out", tag="warm_then_keys", align_bytes=64)
+
+        nc.gpsimd.memset(warm[:], 0.0)
+        nc.vector.memset(ks_pool[:].bitcast(I32), 0)
+        make_identity(nc, ident[:])
+        nc.scalar.activation(warm_out[:], warm[:], ACT.Sigmoid)
+
+        nc.sync.dma_start(key_list[:], offs)
+        nc.sync.dma_start(q_raw[:], qT.rearrange("b (p j) q -> p b j q", j=PACK))
+        nc.sync.dma_start(val_list[:], voffs)
+        for quad in range(4):
+            nc.sync.dma_start(
+                ks_pool[32 * quad : 32 * quad + 4, :].bitcast(I32),
+                k_scales[0, 4 * quad : 4 * quad + 4, :].bitcast(I32),
+            )
+        kw_pool = keep.tile([P, T], U32, name="kw_pool", tag="warm_then_keys", align_bytes=64)
+        nc.sync.dma_start(kw_pool[:].bitcast(I32), k_words[0].rearrange("p t r -> p (t r)").bitcast(I32))
+
+        vb_pool = keep.tile([P, POOL_PAGES * DV], U8, name="vb_pool", tag="warm_then_value_scales", align_bytes=64)
+        nc.vector.memset(vb_pool[:].bitcast(I32), 0)
+
+        q_bf = keep.tile([P, B, NQ, PACK], BF16, name="q_bf", tag="rounded_queries_then_values", align_bytes=64)
+        q_codes = keep.tile([P, B * NQ], U32, name="q_codes", align_bytes=64)
+        q_scale = keep.tile([P, B * NQ], U8, name="q_scale", align_bytes=64)
+        nc.vector.tensor_copy(
+            q_bf[:].rearrange("p b (c i) j -> p b c j i", i=4), q_raw[:].rearrange("p b j (c i) -> p b c j i", i=4)
+        )
+        nc.vector.quantize_mx(
+            out=q_codes[:].bitcast(FP8X4), scales=q_scale[:], in_=q_bf[:].rearrange("p b q j -> p (b q j)")
+        )
+
+        ts_pool = keep.tile([P, T], F32, name="ts_pool", tag="queries_then_token_scales", align_bytes=64)
+        nc.sync.dma_start(ts_pool[:], vs)
+        for quad in range(4):
+            nc.sync.dma_start(
+                vb_pool[32 * quad : 32 * quad + 4, :].bitcast(I32).rearrange("p (u e) -> p u e", u=POOL_PAGES),
+                v_scales[:, 4 * quad : 4 * quad + 4, :].rearrange("u r e -> r u e").bitcast(I32),
+            )
+        vw_pool = keep.tile([P, POOL_PAGES * DV], U32, name="vw_pool", tag="rounded_queries_then_values", align_bytes=64)
+        nc.sync.dma_start(
+            vw_pool[:].bitcast(I32).rearrange("p (u e) -> p u e", u=POOL_PAGES),
+            v_words.rearrange("u p e r -> p u (e r)").bitcast(I32),
+        )
+
+        ks_got = keep.tile([P, B * N], U8, name="ks_got", align_bytes=64)
+        nc.vector.tensor_copy(ks_got[:], ks_pool[:].indirect(key_list[:]))
+
+        def page_offsets(page):
+            return key_list[:, page * PAGE // 16 : (page + 1) * PAGE // 16]
+
+        kw_got = []
+        for page in range(PAGES):
+            got = keep.tile([P, PAGE], U32, name="kw_got%d" % page, align_bytes=64)
+            nc.vector.tensor_copy(got[:], kw_pool[:].indirect(page_offsets(page)))
+            kw_got.append(got)
+
+        probs = []
+        for page in range(PAGES):
+            seq = page * PAGE // N
+            score = psum.tile([P, PAGE], F32, name="score%d" % page)
+            nc.tensor.matmul_mx(
+                out=score[:],
+                lhsT=q_codes[:, seq * NQ : (seq + 1) * NQ].bitcast(FP8X4),
+                lhsT_scale=q_scale[:, seq * NQ : (seq + 1) * NQ],
+                rhs=kw_got[page][:].bitcast(FP8X4),
+                rhs_scale=ks_got[:, page * PAGE : (page + 1) * PAGE],
+                start=True,
+                stop=True,
+            )
+            prob = keep.tile([P, PAGE], F32, name="prob%d" % page, align_bytes=64)
+            nc.scalar.activation(prob[:], score[:], ACT.Sigmoid)
+            probs.append(prob)
+
+        w_bf = []
+        for page in range(PAGES):
+            weight = keep.tile([P, PAGE], F32, name="weight%d" % page, align_bytes=64)
+            nc.vector.tensor_tensor(weight[:], ts_pool[:].indirect(page_offsets(page)), probs[page][:], MULT)
+            turned = psum.tile([P, PACK, NQ], F32, name="turned%d" % (page % 2))
+            for place in range(PACK):
+                nc.tensor.transpose(turned[:, place, :], weight[:, place:PAGE:PACK], ident[:])
+            rounded = keep.tile([P, NQ, PACK], BF16, name="rounded%d" % page, align_bytes=64)
+            nc.scalar.copy(rounded[:], turned[:].rearrange("s t q -> s q t"))
+            w_bf.append(rounded)
+
+        vb_got = keep.tile([P, PAGES * DV], U8, name="vb_got", align_bytes=64)
+        nc.vector.tensor_copy(vb_got[:], vb_pool[:].indirect(val_list[:]))
+
+        per_seq = N // PAGE
+        for seq in range(B):
+            cols = per_seq * DV
+            vw_got = keep.tile([P, cols], U32, name="vw_got%d" % seq, align_bytes=64)
+            nc.vector.tensor_copy(vw_got[:], vw_pool[:].indirect(val_list[:, seq * cols // 16 : (seq + 1) * cols // 16]))
+            acc = psum.tile([P, DV], F32, name="acc%d" % seq)
+            for step in range(per_seq):
+                page = seq * per_seq + step
+                w_codes = keep.tile([P, NQ], U32, name="w_codes%d" % page, align_bytes=64)
+                w_scale = keep.tile([P, NQ], U8, name="w_scale%d" % page, align_bytes=64)
+                nc.vector.quantize_mx(
+                    out=w_codes[:].bitcast(FP8X4), scales=w_scale[:], in_=w_bf[page][:].rearrange("s q t -> s (q t)")
+                )
+                nc.tensor.matmul_mx(
+                    out=acc[:],
+                    lhsT=w_codes[:].bitcast(FP8X4),
+                    lhsT_scale=w_scale[:],
+                    rhs=vw_got[:, step * DV : (step + 1) * DV].bitcast(FP8X4),
+                    rhs_scale=vb_got[:, page * DV : (page + 1) * DV],
+                    start=(step == 0),
+                    stop=(step == per_seq - 1),
+                )
+            result = keep.tile([P, DV], F32, name="result%d" % seq, align_bytes=64)
+            nc.scalar.activation(result[:], acc[:], ACT.Copy, scale=1.0 / 16.0)
+            nc.sync.dma_start(out[seq], result[:])

@@ -31,74 +31,79 @@ def tile_attend_pkv8_sigmoid_kernel(tc, qT, k_words, k_scales, v_words, v_scales
         key_list = keep.tile([P, B * N // 16], U16, name="key_list")
         val_list = keep.tile([P, PAGES * DV // 16], U16, name="val_list")
         ks_pool = keep.tile([P, T], U8, name="ks_pool", align_bytes=64)
-        q_raw = keep.tile([P, B, PACK, NQ], F32, name="q_raw", tag="queries_then_token_scales", align_bytes=64)
+        vb_pool = keep.tile([P, POOL_PAGES * DV], U8, name="vb_pool", align_bytes=64)
         ident = keep.tile([P, P], F32, name="ident", align_bytes=64)
-        warm = keep.tile([P, 8], F32, name="warm", tag="warm_then_value_scales", align_bytes=64)
-        warm_out = keep.tile([P, 8], F32, name="warm_out", tag="warm_then_keys", align_bytes=64)
+        warm = keep.tile([P, 8], F32, name="warm", tag="warm_then_keys", align_bytes=64)
+        warm_out = keep.tile([P, 8], F32, name="warm_out", tag="queries_then_token_scales", align_bytes=64)
 
         nc.gpsimd.memset(warm[:], 0.0)
+        nc.vector.memset(vb_pool[:].bitcast(I32), 0)
         nc.vector.memset(ks_pool[:].bitcast(I32), 0)
-        make_identity(nc, ident[:])
+        nc.vector.memset(ident[:], 0.0)
+        make_identity(nc, ident[:], nomemset=True)
         nc.scalar.activation(warm_out[:], warm[:], ACT.Sigmoid)
 
-        nc.sync.dma_start(key_list[:], offs)
-        nc.sync.dma_start(q_raw[:], qT.rearrange("b (p j) q -> p b j q", j=PACK))
         nc.sync.dma_start(val_list[:], voffs)
+        nc.sync.dma_start(key_list[:], offs)
+        for quad in range(4):
+            nc.sync.dma_start(
+                vb_pool[32 * quad : 32 * quad + 4, :].bitcast(I32).rearrange("p (u e) -> p u e", u=POOL_PAGES),
+                v_scales[:, 4 * quad : 4 * quad + 4, :].rearrange("u r e -> r u e").bitcast(I32),
+            )
         for quad in range(4):
             nc.sync.dma_start(
                 ks_pool[32 * quad : 32 * quad + 4, :].bitcast(I32),
                 k_scales[0, 4 * quad : 4 * quad + 4, :].bitcast(I32),
             )
+        q_raw = keep.tile([P, B, PACK, NQ], F32, name="q_raw", tag="queries_then_token_scales", align_bytes=64)
+        nc.sync.dma_start(q_raw[:], qT.rearrange("b (p j) q -> p b j q", j=PACK))
         kw_pool = keep.tile([P, T], U32, name="kw_pool", tag="warm_then_keys", align_bytes=64)
         nc.sync.dma_start(kw_pool[:].bitcast(I32), k_words[0].rearrange("p t r -> p (t r)").bitcast(I32))
 
-        vb_pool = keep.tile([P, POOL_PAGES * DV], U8, name="vb_pool", tag="warm_then_value_scales", align_bytes=64)
-        nc.vector.memset(vb_pool[:].bitcast(I32), 0)
+        vb_got = keep.tile([P, PAGES * DV], U8, name="vb_got", align_bytes=64)
+        nc.vector.tensor_copy(vb_got[:], vb_pool[:].indirect(val_list[:]))
+
+        ks_got = keep.tile([P, B * N], U8, name="ks_got", align_bytes=64)
+        nc.vector.tensor_copy(ks_got[:], ks_pool[:].indirect(key_list[:]))
 
         q_bf = keep.tile([P, B, NQ, PACK], BF16, name="q_bf", tag="rounded_queries_then_values", align_bytes=64)
         q_codes = keep.tile([P, B * NQ], U32, name="q_codes", align_bytes=64)
         q_scale = keep.tile([P, B * NQ], U8, name="q_scale", align_bytes=64)
-        nc.vector.tensor_copy(
-            q_bf[:].rearrange("p b (c i) j -> p b c j i", i=4), q_raw[:].rearrange("p b j (c i) -> p b c j i", i=4)
-        )
+        for seq in range(B):
+            nc.scalar.copy(
+                q_bf[:, seq].rearrange("p (c i) j -> p c j i", i=4), q_raw[:, seq].rearrange("p j (c i) -> p c j i", i=4)
+            )
         nc.vector.quantize_mx(
             out=q_codes[:].bitcast(FP8X4), scales=q_scale[:], in_=q_bf[:].rearrange("p b q j -> p (b q j)")
         )
 
         ts_pool = keep.tile([P, T], F32, name="ts_pool", tag="queries_then_token_scales", align_bytes=64)
         nc.sync.dma_start(ts_pool[:], vs)
-        for quad in range(4):
-            nc.sync.dma_start(
-                vb_pool[32 * quad : 32 * quad + 4, :].bitcast(I32).rearrange("p (u e) -> p u e", u=POOL_PAGES),
-                v_scales[:, 4 * quad : 4 * quad + 4, :].rearrange("u r e -> r u e").bitcast(I32),
-            )
         vw_pool = keep.tile([P, POOL_PAGES * DV], U32, name="vw_pool", tag="rounded_queries_then_values", align_bytes=64)
         nc.sync.dma_start(
             vw_pool[:].bitcast(I32).rearrange("p (u e) -> p u e", u=POOL_PAGES),
             v_words.rearrange("u p e r -> p u (e r)").bitcast(I32),
         )
 
-        ks_got = keep.tile([P, B * N], U8, name="ks_got", align_bytes=64)
-        nc.vector.tensor_copy(ks_got[:], ks_pool[:].indirect(key_list[:]))
+        def page_offsets(first, count):
+            return key_list[:, first * PAGE // 16 : (first + count) * PAGE // 16]
 
-        def page_offsets(page):
-            return key_list[:, page * PAGE // 16 : (page + 1) * PAGE // 16]
-
+        per_seq = N // PAGE
         kw_got = []
-        for page in range(PAGES):
-            got = keep.tile([P, PAGE], U32, name="kw_got%d" % page, align_bytes=64)
-            nc.vector.tensor_copy(got[:], kw_pool[:].indirect(page_offsets(page)))
+        for seq in range(B):
+            got = keep.tile([P, N], U32, name="kw_got%d" % seq, align_bytes=64)
+            nc.vector.tensor_copy(got[:], kw_pool[:].indirect(page_offsets(seq * per_seq, per_seq)))
             kw_got.append(got)
 
         probs = []
         for page in range(PAGES):
-            seq = page * PAGE // N
+            seq, step = divmod(page, per_seq)
             score = psum.tile([P, PAGE], F32, name="score%d" % page)
             nc.tensor.matmul_mx(
                 out=score[:],
                 lhsT=q_codes[:, seq * NQ : (seq + 1) * NQ].bitcast(FP8X4),
                 lhsT_scale=q_scale[:, seq * NQ : (seq + 1) * NQ],
-                rhs=kw_got[page][:].bitcast(FP8X4),
+                rhs=kw_got[seq][:, step * PAGE : (step + 1) * PAGE].bitcast(FP8X4),
                 rhs_scale=ks_got[:, page * PAGE : (page + 1) * PAGE],
                 start=True,
                 stop=True,
@@ -110,7 +115,7 @@ def tile_attend_pkv8_sigmoid_kernel(tc, qT, k_words, k_scales, v_words, v_scales
         w_bf = []
         for page in range(PAGES):
             weight = keep.tile([P, PAGE], F32, name="weight%d" % page, align_bytes=64)
-            nc.vector.tensor_tensor(weight[:], ts_pool[:].indirect(page_offsets(page)), probs[page][:], MULT)
+            nc.vector.tensor_tensor(weight[:], ts_pool[:].indirect(page_offsets(page, 1)), probs[page][:], MULT)
             turned = psum.tile([P, PACK, NQ], F32, name="turned%d" % (page % 2))
             for place in range(PACK):
                 nc.tensor.transpose(turned[:, place, :], weight[:, place:PAGE:PACK], ident[:])
@@ -118,17 +123,20 @@ def tile_attend_pkv8_sigmoid_kernel(tc, qT, k_words, k_scales, v_words, v_scales
             nc.scalar.copy(rounded[:], turned[:].rearrange("s t q -> s q t"))
             w_bf.append(rounded)
 
-        vb_got = keep.tile([P, PAGES * DV], U8, name="vb_got", align_bytes=64)
-        nc.vector.tensor_copy(vb_got[:], vb_pool[:].indirect(val_list[:]))
+        def gather_values(first, count, tag):
+            got = keep.tile([P, count * DV], U32, name="vw_got%d" % first, tag=tag, align_bytes=64)
+            nc.vector.tensor_copy(
+                got[:], vw_pool[:].indirect(val_list[:, first * DV // 16 : (first + count) * DV // 16])
+            )
+            return [got[:, i * DV : (i + 1) * DV] for i in range(count)]
 
-        per_seq = N // PAGE
+        vw_got = gather_values(0, per_seq, "vw_first") + gather_values(per_seq, 1, "vw_second")
         for seq in range(B):
-            cols = per_seq * DV
-            vw_got = keep.tile([P, cols], U32, name="vw_got%d" % seq, align_bytes=64)
-            nc.vector.tensor_copy(vw_got[:], vw_pool[:].indirect(val_list[:, seq * cols // 16 : (seq + 1) * cols // 16]))
             acc = psum.tile([P, DV], F32, name="acc%d" % seq)
             for step in range(per_seq):
                 page = seq * per_seq + step
+                if page == PAGES - 1:
+                    vw_got.extend(gather_values(page, 1, "weight%d" % page))
                 w_codes = keep.tile([P, NQ], U32, name="w_codes%d" % page, align_bytes=64)
                 w_scale = keep.tile([P, NQ], U8, name="w_scale%d" % page, align_bytes=64)
                 nc.vector.quantize_mx(
@@ -138,7 +146,7 @@ def tile_attend_pkv8_sigmoid_kernel(tc, qT, k_words, k_scales, v_words, v_scales
                     out=acc[:],
                     lhsT=w_codes[:].bitcast(FP8X4),
                     lhsT_scale=w_scale[:],
-                    rhs=vw_got[:, step * DV : (step + 1) * DV].bitcast(FP8X4),
+                    rhs=vw_got[page].bitcast(FP8X4),
                     rhs_scale=vb_got[:, page * DV : (page + 1) * DV],
                     start=(step == 0),
                     stop=(step == per_seq - 1),

@@ -45,6 +45,8 @@ def tile_attend_pkv8_sigmoid_kernel(tc, qT, k_words, k_scales, v_words, v_scales
 
         nc.sync.dma_start(val_list[:], voffs)
         nc.sync.dma_start(key_list[:], offs)
+        ts_rows = keep.tile([P, T // P], F32, name="ts_rows", align_bytes=64)
+        nc.scalar.dma_start(ts_rows[:], vs[0].rearrange("(p c) -> p c", p=P))
         for quad in range(4):
             nc.sync.dma_start(
                 vb_pool[32 * quad : 32 * quad + 4, :].bitcast(I32).rearrange("p (u e) -> p u e", u=POOL_PAGES),
@@ -55,16 +57,37 @@ def tile_attend_pkv8_sigmoid_kernel(tc, qT, k_words, k_scales, v_words, v_scales
                 ks_pool[32 * quad : 32 * quad + 4, :].bitcast(I32),
                 k_scales[0, 4 * quad : 4 * quad + 4, :].bitcast(I32),
             )
-        q_raw = keep.tile([P, B, PACK, NQ], F32, name="q_raw", tag="queries_then_token_scales", align_bytes=64)
-        nc.sync.dma_start(q_raw[:], qT.rearrange("b (p j) q -> p b j q", j=PACK))
         kw_pool = keep.tile([P, T], U32, name="kw_pool", tag="warm_then_keys", align_bytes=64)
         nc.sync.dma_start(kw_pool[:].bitcast(I32), k_words[0].rearrange("p t r -> p (t r)").bitcast(I32))
+        q_raw = keep.tile([P, B, PACK, NQ], F32, name="q_raw", tag="queries_then_token_scales", align_bytes=64)
+        nc.sync.dma_start(q_raw[:], qT.rearrange("b (p j) q -> p b j q", j=PACK))
+
+        ts_pool = keep.tile([P, T], F32, name="ts_pool", align_bytes=64)
+        ts_view = ts_pool[:].rearrange("m (p c) -> m p c", p=P)
+        for group in range(T // P // PACK):
+            spread = psum.tile([P, PACK, P], F32, name="spread", tag="score%d" % (group % PAGES))
+            for j in range(PACK):
+                c = group * PACK + j
+                nc.tensor.transpose(spread[:, j, :], ts_rows[:, c : c + 1].to_broadcast([P, P]), ident[:])
+            nc.scalar.copy(ts_view[:, :, group * PACK : (group + 1) * PACK], spread[:].rearrange("m j p -> m p j"))
 
         vb_got = keep.tile([P, PAGES * DV], U8, name="vb_got", align_bytes=64)
         nc.vector.tensor_copy(vb_got[:], vb_pool[:].indirect(val_list[:]))
 
         ks_got = keep.tile([P, B * N], U8, name="ks_got", align_bytes=64)
         nc.vector.tensor_copy(ks_got[:], ks_pool[:].indirect(key_list[:]))
+
+        def page_offsets(first, count):
+            return key_list[:, first * PAGE // 16 : (first + count) * PAGE // 16]
+
+        per_seq = N // PAGE
+
+        def gather_keys(seq, tag):
+            got = keep.tile([P, N], U32, name="kw_got%d" % seq, tag=tag, align_bytes=64)
+            nc.vector.tensor_copy(got[:], kw_pool[:].indirect(page_offsets(seq * per_seq, per_seq)))
+            return got
+
+        kw_got = [gather_keys(0, "kw_first")]
 
         q_bf = keep.tile([P, B, NQ, PACK], BF16, name="q_bf", tag="rounded_queries_then_values", align_bytes=64)
         q_codes = keep.tile([P, B * NQ], U32, name="q_codes", align_bytes=64)
@@ -77,23 +100,13 @@ def tile_attend_pkv8_sigmoid_kernel(tc, qT, k_words, k_scales, v_words, v_scales
             out=q_codes[:].bitcast(FP8X4), scales=q_scale[:], in_=q_bf[:].rearrange("p b q j -> p (b q j)")
         )
 
-        ts_pool = keep.tile([P, T], F32, name="ts_pool", tag="queries_then_token_scales", align_bytes=64)
-        nc.sync.dma_start(ts_pool[:], vs)
         vw_pool = keep.tile([P, POOL_PAGES * DV], U32, name="vw_pool", tag="rounded_queries_then_values", align_bytes=64)
         nc.sync.dma_start(
             vw_pool[:].bitcast(I32).rearrange("p (u e) -> p u e", u=POOL_PAGES),
             v_words.rearrange("u p e r -> p u (e r)").bitcast(I32),
         )
 
-        def page_offsets(first, count):
-            return key_list[:, first * PAGE // 16 : (first + count) * PAGE // 16]
-
-        per_seq = N // PAGE
-        kw_got = []
-        for seq in range(B):
-            got = keep.tile([P, N], U32, name="kw_got%d" % seq, align_bytes=64)
-            nc.vector.tensor_copy(got[:], kw_pool[:].indirect(page_offsets(seq * per_seq, per_seq)))
-            kw_got.append(got)
+        kw_got.append(gather_keys(1, "queries_then_token_scales"))
 
         probs = []
         for page in range(PAGES):

from contextlib import ExitStack

import concourse.mybir as mybir
from concourse.masks import make_identity

B, N, T, D, DV, NQ = 2, 1024, 4096, 512, 256, 128
PAGE = 512
P = 128
PACK = 4
PAGES = B * N // PAGE
POOL_PAGES = T // PAGE
FLOPS = 2 * B * NQ * N * (D + DV)

F32 = mybir.dt.float32
BF16 = mybir.dt.bfloat16
I32 = mybir.dt.int32
U32 = mybir.dt.uint32
U16 = mybir.dt.uint16
U8 = mybir.dt.uint8
FP8X4 = mybir.dt.float8_e4m3fn_x4
ACT = mybir.ActivationFunctionType
MULT = mybir.AluOpType.mult


def tile_attend_pkv8_sigmoid_kernel(tc, qT, k_words, k_scales, v_words, v_scales, vs, offs, voffs, out):
    nc = tc.nc
    with ExitStack() as ctx:
        keep = ctx.enter_context(tc.tile_pool(name="keep", bufs=1))
        psum = ctx.enter_context(tc.psum_pool(name="psum", bufs=1))

        key_list = keep.tile([P, B * N // 16], U16, name="key_list")
        val_list = keep.tile([P, PAGES * DV // 16], U16, name="val_list")
        ks_pool = keep.tile([P, T], U8, name="ks_pool", align_bytes=64)
        vb_pool = keep.tile([P, POOL_PAGES * DV], U8, name="vb_pool", align_bytes=64)
        ident = keep.tile([P, P], F32, name="ident", align_bytes=64)
        warm = keep.tile([P, 8], F32, name="warm", tag="warm_then_keys", align_bytes=64)
        warm_out = keep.tile([P, 8], F32, name="warm_out", tag="queries_then_token_scales", align_bytes=64)

        nc.gpsimd.memset(warm[:], 0.0)
        nc.vector.memset(vb_pool[:].bitcast(I32), 0)
        nc.vector.memset(ks_pool[:].bitcast(I32), 0)
        nc.vector.memset(ident[:], 0.0)
        make_identity(nc, ident[:], nomemset=True)
        nc.scalar.activation(warm_out[:], warm[:], ACT.Sigmoid)

        nc.sync.dma_start(val_list[:], voffs)
        nc.sync.dma_start(key_list[:], offs)
        ts_rows = keep.tile([P, T // P], F32, name="ts_rows", align_bytes=64)
        nc.scalar.dma_start(ts_rows[:], vs[0].rearrange("(p c) -> p c", p=P))
        for quad in range(4):
            nc.sync.dma_start(
                vb_pool[32 * quad : 32 * quad + 4, :].bitcast(I32).rearrange("p (u e) -> p u e", u=POOL_PAGES),
                v_scales[:, 4 * quad : 4 * quad + 4, :].rearrange("u r e -> r u e").bitcast(I32),
            )
        for quad in range(4):
            nc.sync.dma_start(
                ks_pool[32 * quad : 32 * quad + 4, :].bitcast(I32),
                k_scales[0, 4 * quad : 4 * quad + 4, :].bitcast(I32),
            )
        kw_pool = keep.tile([P, T], U32, name="kw_pool", tag="warm_then_keys", align_bytes=64)
        nc.sync.dma_start(kw_pool[:].bitcast(I32), k_words[0].rearrange("p t r -> p (t r)").bitcast(I32))
        q_raw = keep.tile([P, B, PACK, NQ], F32, name="q_raw", tag="queries_then_token_scales", align_bytes=64)
        nc.sync.dma_start(q_raw[:], qT.rearrange("b (p j) q -> p b j q", j=PACK))

        ts_pool = keep.tile([P, T], F32, name="ts_pool", align_bytes=64)
        ts_view = ts_pool[:].rearrange("m (p c) -> m p c", p=P)
        for group in range(T // P // PACK):
            spread = psum.tile([P, PACK, P], F32, name="spread", tag="score%d" % (group % PAGES))
            for j in range(PACK):
                c = group * PACK + j
                nc.tensor.transpose(spread[:, j, :], ts_rows[:, c : c + 1].to_broadcast([P, P]), ident[:])
            nc.scalar.copy(ts_view[:, :, group * PACK : (group + 1) * PACK], spread[:].rearrange("m j p -> m p j"))

        vb_got = keep.tile([P, PAGES * DV], U8, name="vb_got", align_bytes=64)
        nc.vector.tensor_copy(vb_got[:], vb_pool[:].indirect(val_list[:]))

        ks_got = keep.tile([P, B * N], U8, name="ks_got", align_bytes=64)
        nc.vector.tensor_copy(ks_got[:], ks_pool[:].indirect(key_list[:]))

        def page_offsets(first, count):
            return key_list[:, first * PAGE // 16 : (first + count) * PAGE // 16]

        per_seq = N // PAGE

        def gather_keys(seq, tag):
            got = keep.tile([P, N], U32, name="kw_got%d" % seq, tag=tag, align_bytes=64)
            nc.vector.tensor_copy(got[:], kw_pool[:].indirect(page_offsets(seq * per_seq, per_seq)))
            return got

        kw_got = [gather_keys(0, "kw_first")]

        q_bf = keep.tile([P, B, NQ, PACK], BF16, name="q_bf", tag="rounded_queries_then_values", align_bytes=64)
        q_codes = keep.tile([P, B * NQ], U32, name="q_codes", align_bytes=64)
        q_scale = keep.tile([P, B * NQ], U8, name="q_scale", align_bytes=64)
        for seq in range(B):
            nc.scalar.copy(
                q_bf[:, seq].rearrange("p (c i) j -> p c j i", i=4), q_raw[:, seq].rearrange("p j (c i) -> p c j i", i=4)
            )
        nc.vector.quantize_mx(
            out=q_codes[:].bitcast(FP8X4), scales=q_scale[:], in_=q_bf[:].rearrange("p b q j -> p (b q j)")
        )

        vw_pool = keep.tile([P, POOL_PAGES * DV], U32, name="vw_pool", tag="rounded_queries_then_values", align_bytes=64)
        nc.sync.dma_start(
            vw_pool[:].bitcast(I32).rearrange("p (u e) -> p u e", u=POOL_PAGES),
            v_words.rearrange("u p e r -> p u (e r)").bitcast(I32),
        )

        kw_got.append(gather_keys(1, "queries_then_token_scales"))

        probs = []
        for page in range(PAGES):
            seq, step = divmod(page, per_seq)
            score = psum.tile([P, PAGE], F32, name="score%d" % page)
            nc.tensor.matmul_mx(
                out=score[:],
                lhsT=q_codes[:, seq * NQ : (seq + 1) * NQ].bitcast(FP8X4),
                lhsT_scale=q_scale[:, seq * NQ : (seq + 1) * NQ],
                rhs=kw_got[seq][:, step * PAGE : (step + 1) * PAGE].bitcast(FP8X4),
                rhs_scale=ks_got[:, page * PAGE : (page + 1) * PAGE],
                start=True,
                stop=True,
            )
            prob = keep.tile([P, PAGE], F32, name="prob%d" % page, align_bytes=64)
            nc.scalar.activation(prob[:], score[:], ACT.Sigmoid)
            probs.append(prob)

        w_bf = []
        for page in range(PAGES):
            weight = keep.tile([P, PAGE], F32, name="weight%d" % page, align_bytes=64)
            nc.vector.tensor_tensor(weight[:], ts_pool[:].indirect(page_offsets(page, 1)), probs[page][:], MULT)
            turned = psum.tile([P, PACK, NQ], F32, name="turned%d" % (page % 2))
            for place in range(PACK):
                nc.tensor.transpose(turned[:, place, :], weight[:, place:PAGE:PACK], ident[:])
            rounded = keep.tile([P, NQ, PACK], BF16, name="rounded%d" % page, align_bytes=64)
            nc.scalar.copy(rounded[:], turned[:].rearrange("s t q -> s q t"))
            w_bf.append(rounded)

        def gather_values(first, count, tag):
            got = keep.tile([P, count * DV], U32, name="vw_got%d" % first, tag=tag, align_bytes=64)
            nc.vector.tensor_copy(
                got[:], vw_pool[:].indirect(val_list[:, first * DV // 16 : (first + count) * DV // 16])
            )
            return [got[:, i * DV : (i + 1) * DV] for i in range(count)]

        vw_got = gather_values(0, per_seq, "vw_first") + gather_values(per_seq, 1, "vw_second")
        for seq in range(B):
            acc = psum.tile([P, DV], F32, name="acc%d" % seq)
            for step in range(per_seq):
                page = seq * per_seq + step
                if page == PAGES - 1:
                    vw_got.extend(gather_values(page, 1, "weight%d" % page))
                w_codes = keep.tile([P, NQ], U32, name="w_codes%d" % page, align_bytes=64)
                w_scale = keep.tile([P, NQ], U8, name="w_scale%d" % page, align_bytes=64)
                nc.vector.quantize_mx(
                    out=w_codes[:].bitcast(FP8X4), scales=w_scale[:], in_=w_bf[page][:].rearrange("s q t -> s (q t)")
                )
                nc.tensor.matmul_mx(
                    out=acc[:],
                    lhsT=w_codes[:].bitcast(FP8X4),
                    lhsT_scale=w_scale[:],
                    rhs=vw_got[page].bitcast(FP8X4),
                    rhs_scale=vb_got[:, page * DV : (page + 1) * DV],
                    start=(step == 0),
                    stop=(step == per_seq - 1),
                )
            result = keep.tile([P, DV], F32, name="result%d" % seq, align_bytes=64)
            nc.scalar.activation(result[:], acc[:], ACT.Copy, scale=1.0 / 16.0)
            nc.sync.dma_start(out[seq], result[:])
